import numpy as np
import ml_dtypes


def mxq(x, axis, fmt="e4m3"):
    dtype, down = {"e4m3": (ml_dtypes.float8_e4m3fn, 7), "e5m2": (ml_dtypes.float8_e5m2, 14)}[fmt]
    v = np.moveaxis(np.asarray(x, np.float32).astype(ml_dtypes.bfloat16).astype(np.float64), axis, -1)
    blocks = v.reshape(v.shape[:-1] + (-1, 32))
    amax = np.abs(blocks).max(-1, keepdims=True)
    byte = np.maximum(np.where(amax > 0, np.frexp(amax)[1] - 1 + 127, 0) - down, 1)
    scale = np.exp2(byte - 127.0)
    codes = (blocks / scale).astype(np.float32).astype(dtype).astype(np.float64)
    return np.moveaxis((codes * scale).reshape(v.shape), -1, axis)


WIDE = False


def mx_kscale(k):
    if not WIDE:
        return np.ones(k)
    levels = np.array([10, -10, 5, -5, 0])
    if k % 512:
        return np.exp2(np.random.permutation(np.resize(levels, k // 32))).repeat(32)
    a = np.empty((k // 512, 16))
    for p in range(k // 512):
        a[p, :8] = np.random.permutation(np.resize(levels, 8))
        for g in range(8):
            far = levels[np.abs(levels - a[p, g]) >= 10]
            a[p, g + 8] = far[np.random.randint(len(far))]
    return np.exp2(a.ravel()).repeat(32)


def f64(x):
    return np.asarray(x).astype(np.float64)


def striped(idx):
    return np.tile(np.asarray(idx).reshape(-1, 16).T, (8, 1)).astype(np.uint16)


def unstriped(offs):
    return offs[:16].T.reshape(-1).astype(np.int64)


E2M1 = np.array([0.0, 0.5, 1.0, 1.5, 2.0, 3.0, 4.0, 6.0, -0.0, -0.5, -1.0, -1.5, -2.0, -3.0, -4.0, -6.0])


def pack_weight(w, fmt):
    k, n = w.shape
    w = f64(np.asarray(w, np.float32).astype(ml_dtypes.bfloat16)).reshape(k // 32, 32, n)
    amax = np.abs(w).max(1)
    if fmt == "e4m3":
        byte = np.frexp(amax)[1] - 1 + 127 - 7
    else:
        mant, ex = np.frexp(amax / 6.0)
        byte = np.where(mant > 0.5, ex, ex - 1) + 127
    byte = np.clip(np.where(amax > 0, byte, 1), 1, 254)
    scaled = (w * np.exp2(127.0 - byte)[:, None, :]).reshape(k, n).astype(np.float32)
    by_word = np.ascontiguousarray(scaled.reshape(k // 512, 128, 4, n).transpose(0, 1, 3, 2))
    if fmt == "e4m3":
        words = by_word.astype(ml_dtypes.float8_e4m3fn).view(np.uint8)
    else:
        c = by_word.astype(ml_dtypes.float4_e2m1fn).view(np.uint8) & 0xF
        words = (c[..., 0::2] | (c[..., 1::2] << 4)).reshape(k // 512, 128, 2 * n)
    return np.ascontiguousarray(words), np.ascontiguousarray(byte.astype(np.uint8).reshape(k // 512, 16, n))


def unpack_weight(words, scales, fmt):
    g, _, n = scales.shape
    words = np.ascontiguousarray(words).reshape(g, 128, n, -1)
    if fmt == "e4m3":
        vals = words.view(ml_dtypes.float8_e4m3fn).astype(np.float64)
    else:
        nib = np.empty((g, 128, n, 4), np.uint8)
        nib[..., 0::2] = words & 0xF
        nib[..., 1::2] = words >> 4
        vals = E2M1[nib]
    vals = vals * np.repeat(np.exp2(scales.astype(np.float64) - 127.0), 8, axis=1)[..., None]
    return vals.transpose(0, 1, 3, 2).reshape(g * 512, n)


def bf(x):
    return np.asarray(x, np.float32).astype(ml_dtypes.bfloat16)


def planes(Y):
    r, m = Y.shape
    b = f64(bf(Y)).reshape(r // 32, 32, m)
    amax = np.abs(b).max(1)
    byte = np.clip(np.where(amax > 0, np.frexp(amax)[1] - 1 + 127 - 7, 1), 1, 254)
    codes = (b * np.exp2(127.0 - byte)[:, None, :]).reshape(r, m).astype(np.float32).astype(ml_dtypes.float8_e4m3fn).view(np.uint8)
    words = codes.reshape(r // 512, 128, 4, m).transpose(0, 1, 3, 2)
    return np.ascontiguousarray(words), np.ascontiguousarray(byte.astype(np.uint8).reshape(r // 512, 16, m))


K, T, J, B, N = 512, 2048, 1024, 256, 512


def setup_inputs():
    n = np.random.standard_normal
    idx = np.random.permutation(T)[:J]
    fk = mx_kscale(K)
    wgp = pack_weight(n((K, N)) * 1 / np.sqrt(K) * fk[:, None], "e4m3")
    xqp = pack_weight(n((K, J)) / fk[:, None], "e2m1")
    wmp = pack_weight(n((K, N)) * 1 / np.sqrt(K) * fk[:, None], "e4m3")
    return {
        "xf": (n((K, T)) / fk[:, None]).astype(np.float32),
        "wg_words": wgp[0],
        "wg_scales": wgp[1],
        "xq_words": xqp[0],
        "xq_scales": xqp[1],
        "wm_words": wmp[0],
        "wm_scales": wmp[1],
        "offs": striped(idx),
    }


def reference(xf, wg_words, wg_scales, xq_words, xq_scales, wm_words, wm_scales, offs):
    idx = unstriped(offs)
    wgu = unpack_weight(wg_words, wg_scales, "e4m3")
    xqu = unpack_weight(xq_words, xq_scales, "e2m1")
    wmu = unpack_weight(wm_words, wm_scales, "e4m3")
    m = f64(xf)[:, idx].reshape(K, B, J // B).mean(axis=2)
    mf = 2.0 * m
    mfq = mxq(mf, 0, "e4m3")
    zg = wgu.T @ mfq
    zm = wmu.T @ xqu
    zr = np.repeat(zg, J // B, axis=1)
    y = zm + zr
    words, scales = planes(y)
    return y, words, scales

@@ -1,0 +1,205 @@
+from contextlib import ExitStack
+
+import concourse.mybir as mybir
+from concourse.masks import make_identity
+
+K, T, J, B, N = 512, 2048, 1024, 256, 512
+FLOPS = 2 * K * N * (J + B)
+
+F32 = mybir.dt.float32
+BF16 = mybir.dt.bfloat16
+I32 = mybir.dt.int32
+U16 = mybir.dt.uint16
+U8 = mybir.dt.uint8
+FP8X4 = mybir.dt.float8_e4m3fn_x4
+FP4X4 = mybir.dt.float4_e2m1fn_x4
+ADD = mybir.AluOpType.add
+COPY = mybir.ActivationFunctionType.Copy
+AXIS_X = mybir.AxisListType.X
+
+P = 128
+PACK = 4
+MEMBERS = J // B
+HALF = B // 2
+QUARTER = B // 4
+CHUNK = 128
+ZM_BANKS = [("zm", 2), ("zm", 2), ("turned", 2), ("turned", 2), ("back", 1), ("zm", 2), ("zm", 2), ("turned", 2)]
+
+
+def load_scale_rows(queue, plane, scales):
+    for quad in range(4):
+        queue.dma_start(
+            out=plane[32 * quad : 32 * quad + 4, :].bitcast(I32),
+            in_=scales[0, 4 * quad : 4 * quad + 4, :].bitcast(I32),
+        )
+
+
+def tile_list_group_mean_and_members_pl_kernel(
+    tc, xf, wg_words, wg_scales, xq_words, xq_scales, wm_words, wm_scales, offs, out_0, out_1, out_2
+):
+    nc = tc.nc
+    with ExitStack() as ctx:
+        held = ctx.enter_context(tc.tile_pool(name="held", bufs=1))
+        psum = ctx.enter_context(tc.psum_pool(name="psum", bufs=1))
+
+        offsets = held.tile([P, J // 16], U16, name="offsets")
+        nc.sync.dma_start(offsets[:], offs)
+
+        w_sraw = held.tile([P, 2 * N], U8, name="w_sraw")
+        xq_plane = held.tile([P, J], U8, name="xq_plane", align_bytes=64)
+        nc.gpsimd.memset(w_sraw[:].bitcast(I32), 0)
+        nc.gpsimd.memset(xq_plane[:].bitcast(I32), 0)
+        ident = held.tile([P, P], F32, name="ident")
+        make_identity(nc, ident[:])
+
+        x_rows = xf.rearrange("(p t) c -> p t c", t=PACK)
+        x = [held.tile([P, T], F32, name="x%d" % t, align_bytes=64) for t in range(PACK)]
+        wm_raw = held.tile([P, N], I32, name="wm_raw", align_bytes=64)
+        wg_raw = held.tile([P, N], I32, name="wg_raw")
+        xq = held.tile([P, 2 * J], U8, name="xq", align_bytes=64)
+
+        nc.sync.dma_start(out=x[0][:], in_=x_rows[:, 0, :])
+        load_scale_rows(nc.sync, w_sraw[:, 0:N], wm_scales)
+        nc.sync.dma_start(out=x[1][:], in_=x_rows[:, 1, :])
+        nc.sync.dma_start(out=wm_raw[:], in_=wm_words[0].rearrange("p n t -> p (n t)").bitcast(I32))
+        load_scale_rows(nc.sync, w_sraw[:, N : 2 * N], wg_scales)
+        nc.sync.dma_start(out=xq[:].bitcast(I32), in_=xq_words[0].bitcast(I32))
+        nc.sync.dma_start(out=x[2][:], in_=x_rows[:, 2, :])
+        load_scale_rows(nc.sync, xq_plane[:], xq_scales)
+        nc.sync.dma_start(out=x[3][:], in_=x_rows[:, 3, :])
+        nc.sync.dma_start(out=wg_raw[:], in_=wg_words[0].rearrange("p n t -> p (n t)").bitcast(I32))
+
+        def deal(raw, dtype, name, tag):
+            dealt = held.tile([P, PACK, P], dtype, name=name, tag=tag, align_bytes=64)
+            nc.vector.tensor_copy(out=dealt[:], in_=raw[:].rearrange("p (m t) -> p t m", t=PACK))
+            return dealt
+
+        sums = [held.tile([P, 2, PACK, QUARTER], F32, name="sums%d" % h) for h in range(2)]
+
+        def sum_on_tensor(t, h):
+            name = "picked%d%d" % (t, h)
+            tag = "wm_raw" if (t, h) == (2, 0) else name
+            picked = held.tile([P, HALF, MEMBERS], F32, name=name, tag=tag, align_bytes=64)
+            cols = HALF * MEMBERS // 16
+            nc.vector.tensor_copy(
+                out=picked[:].rearrange("p b i -> p (b i)"),
+                in_=x[t][:].indirect(offsets[:, h * cols : (h + 1) * cols]),
+            )
+            turned = psum.tile([P, P], F32, name="turned", bufs=2)
+            for i in range(MEMBERS):
+                nc.tensor.matmul(
+                    turned[:], picked[:, :, i], ident[:], start=(i == 0), stop=(i == MEMBERS - 1), is_transpose=True
+                )
+            turned_sb = held.tile([P, P], F32, name="turned_sb%d%d" % (t, h))
+            nc.scalar.activation(out=turned_sb[:], in_=turned[:], func=COPY)
+            back = psum.tile([P, P], F32, name="back", bufs=1)
+            nc.tensor.transpose(back[:], turned_sb[:], ident[:])
+            nc.scalar.copy(out=sums[h][:, :, t, :], in_=back[:].rearrange("p (q b) -> p q b", q=2))
+
+        for h in range(2):
+            sum_on_tensor(0, h)
+        for h in range(2):
+            sum_on_tensor(1, h)
+        wm = deal(wm_raw, I32, "wm", "x1")
+        w_planes = held.tile([P, 2, PACK, P], U8, name="w_planes", tag="picked01", align_bytes=64)
+        nc.vector.tensor_copy(out=w_planes[:], in_=w_sraw[:].rearrange("p (w m t) -> p w t m", w=2, t=PACK))
+        for h in range(2):
+            sum_on_tensor(2, h)
+
+        def member_products(c):
+            tag, bufs = ZM_BANKS[c]
+            zm = psum.tile([P, PACK, CHUNK], F32, name="zm%d" % c, tag=tag, bufs=bufs)
+            for t in range(PACK):
+                nc.tensor.matmul_mx(
+                    out=zm[:, t, :],
+                    lhsT=wm[:, t, :].bitcast(FP8X4),
+                    lhsT_scale=w_planes[:, 0, t, :],
+                    rhs=xq[:, 2 * CHUNK * c : 2 * CHUNK * (c + 1)].bitcast(FP4X4),
+                    rhs_scale=xq_plane[:, CHUNK * c : CHUNK * (c + 1)],
+                    start=True,
+                    stop=True,
+                )
+            return zm
+
+        def pick_last(q):
+            tag = "mf0" if q == 3 else "last%d" % q
+            picked = held.tile([P, QUARTER, MEMBERS], F32, name="last%d" % q, tag=tag, align_bytes=64)
+            cols = QUARTER * MEMBERS // 16
+            nc.vector.tensor_copy(
+                out=picked[:].rearrange("p b i -> p (b i)"),
+                in_=x[3][:].indirect(offsets[:, q * cols : (q + 1) * cols]),
+            )
+            nc.vector.tensor_reduce(out=sums[q // 2][:, q % 2, 3, :], in_=picked[:], axis=AXIS_X, op=ADD)
+            mf = held.tile([P, QUARTER, PACK], BF16, name="mf%d" % q, align_bytes=64)
+            nc.scalar.activation(
+                out=mf[:], in_=sums[q // 2][:, q % 2, :, :].rearrange("p t b -> p b t"), func=COPY, scale=2.0 / MEMBERS
+            )
+            return mf
+
+        def group_products(q, mf):
+            codes = held.tile([P, QUARTER], I32, name="mf_codes%d" % q, align_bytes=64)
+            plane = held.tile([P, QUARTER], U8, name="mf_plane%d" % q, align_bytes=64)
+            nc.vector.quantize_mx(
+                out=codes[:].bitcast(FP8X4), scales=plane[:], in_=mf[:].rearrange("p b t -> p (b t)")
+            )
+            zg = psum.tile([P, PACK, QUARTER], F32, name="zg", bufs=2)
+            for t in range(PACK):
+                nc.tensor.matmul_mx(
+                    out=zg[:, t, :],
+                    lhsT=wg[:, t, :].bitcast(FP8X4),
+                    lhsT_scale=w_planes[:, 1, t, :],
+                    rhs=codes[:].bitcast(FP8X4),
+                    rhs_scale=plane[:],
+                    start=True,
+                    stop=True,
+                )
+            staged = held.tile([P, PACK, QUARTER], F32, name="zg_sb%d" % q)
+            nc.scalar.copy(out=staged[:], in_=zg[:])
+            return staged
+
+        mf0 = pick_last(0)
+        mf1 = pick_last(1)
+        wg = deal(wg_raw, I32, "wg", "last1")
+        zg_sb = [group_products(0, mf0)]
+        mf2 = pick_last(2)
+        zg_sb.append(group_products(1, mf1))
+        mf3 = pick_last(3)
+        zg_sb.append(group_products(2, mf2))
+        zg_sb.append(group_products(3, mf3))
+
+        y_rows = out_0.rearrange("(p t) j -> p t j", t=PACK)
+        word_rows = out_1[0].rearrange("p c r -> p (c r)").bitcast(I32)
+        y_plane = held.tile([P, J], U8, name="y_plane", align_bytes=64)
+        groups = CHUNK // MEMBERS
+        for q in range(4):
+            y = held.tile([P, 2, PACK, CHUNK], F32, name="y%d" % q)
+            y_codes = held.tile([P, 2 * CHUNK], I32, name="y_codes%d" % q, align_bytes=64)
+            for s in range(2):
+                c = 2 * q + s
+                zm = member_products(c)
+                nc.vector.tensor_tensor(
+                    out=y[:, s, :, :].rearrange("p t (b i) -> p t b i", i=MEMBERS),
+                    in0=zm[:].rearrange("p t (b i) -> p t b i", i=MEMBERS),
+                    in1=zg_sb[q][:, :, s * groups : (s + 1) * groups]
+                    .unsqueeze(3)
+                    .to_broadcast([P, PACK, groups, MEMBERS]),
+                    op=ADD,
+                )
+                nc.sync.dma_start(out=y_rows[:, :, CHUNK * c : CHUNK * (c + 1)], in_=y[:, s, :, :])
+                rounded = held.tile([P, CHUNK, PACK], BF16, name="rounded%d" % c, align_bytes=64)
+                nc.scalar.copy(
+                    out=rounded[:].rearrange("p (g i) t -> p g t i", i=4),
+                    in_=y[:, s, :, :].rearrange("p t (g i) -> p g t i", i=4),
+                )
+                nc.vector.quantize_mx(
+                    out=y_codes[:, s * CHUNK : (s + 1) * CHUNK].bitcast(FP8X4),
+                    scales=y_plane[:, CHUNK * c : CHUNK * (c + 1)],
+                    in_=rounded[:].rearrange("p j t -> p (j t)"),
+                )
+            nc.sync.dma_start(out=word_rows[:, 2 * CHUNK * q : 2 * CHUNK * (q + 1)], in_=y_codes[:])
+        for quad in range(4):
+            queue = nc.sync if quad % 2 == 0 else nc.scalar
+            queue.dma_start(
+                out=out_2[0, 4 * quad : 4 * quad + 4, :].bitcast(I32),
+                in_=y_plane[32 * quad : 32 * quad + 4, :].bitcast(I32),
+            )

@@ -23,7 +23,7 @@ MEMBERS = J // B
 HALF = B // 2
 QUARTER = B // 4
 CHUNK = 128
-ZM_BANKS = [("zm", 2), ("zm", 2), ("turned", 2), ("turned", 2), ("back", 1), ("zm", 2), ("zm", 2), ("turned", 2)]
+BANKS = {"turned": 3, "zm": 2, "zg": 2}
 
 
 def load_scale_rows(queue, plane, scales):
@@ -45,36 +45,42 @@ def tile_list_group_mean_and_members_pl_kernel(
         offsets = held.tile([P, J // 16], U16, name="offsets")
         nc.sync.dma_start(offsets[:], offs)
 
-        w_sraw = held.tile([P, 2 * N], U8, name="w_sraw")
+        wg_sraw = held.tile([P, N], U8, name="wg_sraw", align_bytes=64)
+        wm_sraw = held.tile([P, N], U8, name="wm_sraw", align_bytes=64)
         xq_plane = held.tile([P, J], U8, name="xq_plane", align_bytes=64)
-        nc.gpsimd.memset(w_sraw[:].bitcast(I32), 0)
-        nc.gpsimd.memset(xq_plane[:].bitcast(I32), 0)
+        for plane in (wm_sraw, wg_sraw, xq_plane):
+            nc.gpsimd.memset(plane[:].bitcast(I32), 0)
         ident = held.tile([P, P], F32, name="ident")
         make_identity(nc, ident[:])
 
         x_rows = xf.rearrange("(p t) c -> p t c", t=PACK)
         x = [held.tile([P, T], F32, name="x%d" % t, align_bytes=64) for t in range(PACK)]
         wm_raw = held.tile([P, N], I32, name="wm_raw", align_bytes=64)
-        wg_raw = held.tile([P, N], I32, name="wg_raw")
+        wg_raw = held.tile([P, N], I32, name="wg_raw", align_bytes=64)
         xq = held.tile([P, 2 * J], U8, name="xq", align_bytes=64)
 
         nc.sync.dma_start(out=x[0][:], in_=x_rows[:, 0, :])
-        load_scale_rows(nc.sync, w_sraw[:, 0:N], wm_scales)
+        load_scale_rows(nc.sync, wm_sraw, wm_scales)
         nc.sync.dma_start(out=x[1][:], in_=x_rows[:, 1, :])
         nc.sync.dma_start(out=wm_raw[:], in_=wm_words[0].rearrange("p n t -> p (n t)").bitcast(I32))
-        load_scale_rows(nc.sync, w_sraw[:, N : 2 * N], wg_scales)
+        load_scale_rows(nc.sync, wg_sraw, wg_scales)
         nc.sync.dma_start(out=xq[:].bitcast(I32), in_=xq_words[0].bitcast(I32))
         nc.sync.dma_start(out=x[2][:], in_=x_rows[:, 2, :])
-        load_scale_rows(nc.sync, xq_plane[:], xq_scales)
+        load_scale_rows(nc.sync, xq_plane, xq_scales)
         nc.sync.dma_start(out=x[3][:], in_=x_rows[:, 3, :])
         nc.sync.dma_start(out=wg_raw[:], in_=wg_words[0].rearrange("p n t -> p (n t)").bitcast(I32))
 
         def deal(raw, dtype, name, tag):
             dealt = held.tile([P, PACK, P], dtype, name=name, tag=tag, align_bytes=64)
-            nc.vector.tensor_copy(out=dealt[:], in_=raw[:].rearrange("p (m t) -> p t m", t=PACK))
+            if dtype == U8:
+                nc.vector.tensor_copy(out=dealt[:], in_=raw[:].rearrange("p (m t) -> p t m", t=PACK))
+            else:
+                nc.vector.tensor_copy(
+                    out=dealt[:].rearrange("p t m -> p m t"), in_=raw[:].rearrange("p (m t) -> p m t", t=PACK)
+                )
             return dealt
 
-        sums = [held.tile([P, 2, PACK, QUARTER], F32, name="sums%d" % h) for h in range(2)]
+        sums = [held.tile([P, PACK, HALF], F32, name="sums%d" % h) for h in range(2)]
 
         def sum_on_tensor(t, h):
             name = "picked%d%d" % (t, h)
@@ -85,37 +91,43 @@ def tile_list_group_mean_and_members_pl_kernel(
                 out=picked[:].rearrange("p b i -> p (b i)"),
                 in_=x[t][:].indirect(offsets[:, h * cols : (h + 1) * cols]),
             )
-            turned = psum.tile([P, P], F32, name="turned", bufs=2)
+            by_member = picked[:].rearrange("p b i -> p i b")
+            if t < 2:
+                parted = held.tile([P, MEMBERS, HALF], F32, name="parted%d%d" % (t, h))
+                nc.scalar.copy(out=parted[:].rearrange("p i b -> p b i"), in_=picked[:])
+                by_member = parted[:]
+            turned = psum.tile([P, P], F32, name="turned", bufs=3)
             for i in range(MEMBERS):
                 nc.tensor.matmul(
-                    turned[:], picked[:, :, i], ident[:], start=(i == 0), stop=(i == MEMBERS - 1), is_transpose=True
+                    turned[:], by_member[:, i, :], ident[:], start=(i == 0), stop=(i == MEMBERS - 1), is_transpose=True
                 )
             turned_sb = held.tile([P, P], F32, name="turned_sb%d%d" % (t, h))
             nc.scalar.activation(out=turned_sb[:], in_=turned[:], func=COPY)
-            back = psum.tile([P, P], F32, name="back", bufs=1)
-            nc.tensor.transpose(back[:], turned_sb[:], ident[:])
-            nc.scalar.copy(out=sums[h][:, :, t, :], in_=back[:].rearrange("p (q b) -> p q b", q=2))
+            return turned_sb
 
-        for h in range(2):
-            sum_on_tensor(0, h)
-        for h in range(2):
-            sum_on_tensor(1, h)
+        def turn_back(h, planes):
+            back = psum.tile([P, PACK - 1, P], F32, name="back%d" % h, tag="turned", bufs=3)
+            for t in range(PACK - 1):
+                nc.tensor.transpose(back[:, t, :], planes[t][:], ident[:])
+            nc.scalar.copy(out=sums[h][:, 0 : PACK - 1, :], in_=back[:])
+
+        early = [[sum_on_tensor(t, h) for h in range(2)] for t in range(2)]
+        wm_plane = deal(wm_sraw, U8, "wm_plane", "x0")
         wm = deal(wm_raw, I32, "wm", "x1")
-        w_planes = held.tile([P, 2, PACK, P], U8, name="w_planes", tag="picked01", align_bytes=64)
-        nc.vector.tensor_copy(out=w_planes[:], in_=w_sraw[:].rearrange("p (w m t) -> p w t m", w=2, t=PACK))
+        wg_plane = deal(wg_sraw, U8, "wg_plane", "picked01")
         for h in range(2):
-            sum_on_tensor(2, h)
+            turn_back(h, [early[0][h], early[1][h], sum_on_tensor(2, h)])
 
-        def member_products(c):
-            tag, bufs = ZM_BANKS[c]
-            zm = psum.tile([P, PACK, CHUNK], F32, name="zm%d" % c, tag=tag, bufs=bufs)
-            for t in range(PACK):
+        def member_products(slices, cols, tag):
+            width = cols.stop - cols.start
+            zm = psum.tile([P, len(slices), width], F32, name="zm", tag=tag, bufs=BANKS[tag])
+            for k, t in enumerate(slices):
                 nc.tensor.matmul_mx(
-                    out=zm[:, t, :],
+                    out=zm[:, k, :],
                     lhsT=wm[:, t, :].bitcast(FP8X4),
-                    lhsT_scale=w_planes[:, 0, t, :],
-                    rhs=xq[:, 2 * CHUNK * c : 2 * CHUNK * (c + 1)].bitcast(FP4X4),
-                    rhs_scale=xq_plane[:, CHUNK * c : CHUNK * (c + 1)],
+                    lhsT_scale=wm_plane[:, t, :],
+                    rhs=xq[:, 2 * cols.start : 2 * cols.stop].bitcast(FP4X4),
+                    rhs_scale=xq_plane[:, cols],
                     start=True,
                     stop=True,
                 )
@@ -129,25 +141,26 @@ def tile_list_group_mean_and_members_pl_kernel(
                 out=picked[:].rearrange("p b i -> p (b i)"),
                 in_=x[3][:].indirect(offsets[:, q * cols : (q + 1) * cols]),
             )
-            nc.vector.tensor_reduce(out=sums[q // 2][:, q % 2, 3, :], in_=picked[:], axis=AXIS_X, op=ADD)
+            mine = slice(QUARTER * (q % 2), QUARTER * (q % 2 + 1))
+            nc.vector.tensor_reduce(out=sums[q // 2][:, 3, mine], in_=picked[:], axis=AXIS_X, op=ADD)
             mf = held.tile([P, QUARTER, PACK], BF16, name="mf%d" % q, align_bytes=64)
             nc.scalar.activation(
-                out=mf[:], in_=sums[q // 2][:, q % 2, :, :].rearrange("p t b -> p b t"), func=COPY, scale=2.0 / MEMBERS
+                out=mf[:], in_=sums[q // 2][:, :, mine].rearrange("p t b -> p b t"), func=COPY, scale=2.0 / MEMBERS
             )
             return mf
 
-        def group_products(q, mf):
+        def group_products(q, mf, bank):
             codes = held.tile([P, QUARTER], I32, name="mf_codes%d" % q, align_bytes=64)
             plane = held.tile([P, QUARTER], U8, name="mf_plane%d" % q, align_bytes=64)
             nc.vector.quantize_mx(
                 out=codes[:].bitcast(FP8X4), scales=plane[:], in_=mf[:].rearrange("p b t -> p (b t)")
             )
-            zg = psum.tile([P, PACK, QUARTER], F32, name="zg", bufs=2)
+            zg = psum.tile([P, PACK, QUARTER], F32, name="zg", tag=bank, bufs=BANKS[bank])
             for t in range(PACK):
                 nc.tensor.matmul_mx(
                     out=zg[:, t, :],
                     lhsT=wg[:, t, :].bitcast(FP8X4),
-                    lhsT_scale=w_planes[:, 1, t, :],
+                    lhsT_scale=wg_plane[:, t, :],
                     rhs=codes[:].bitcast(FP8X4),
                     rhs_scale=plane[:],
                     start=True,
@@ -157,46 +170,68 @@ def tile_list_group_mean_and_members_pl_kernel(
             nc.scalar.copy(out=staged[:], in_=zg[:])
             return staged
 
+        wide = 2 * CHUNK
+        parts = [((2 * u, 2 * u + 1), slice(wide * q, wide * (q + 1))) for q in range(3) for u in range(2)]
+        parts = parts + [(range(PACK), slice(3 * wide + CHUNK * s, 3 * wide + CHUNK * (s + 1))) for s in range(2)]
+        zm = [member_products(*parts[k], "zm") for k in range(2)]
         mf0 = pick_last(0)
         mf1 = pick_last(1)
         wg = deal(wg_raw, I32, "wg", "last1")
-        zg_sb = [group_products(0, mf0)]
+        zg_sb = [group_products(0, mf0, "turned")]
         mf2 = pick_last(2)
-        zg_sb.append(group_products(1, mf1))
+        zg_sb.append(group_products(1, mf1, "turned"))
         mf3 = pick_last(3)
-        zg_sb.append(group_products(2, mf2))
-        zg_sb.append(group_products(3, mf3))
+        zg_sb.append(group_products(2, mf2, "zg"))
+        zg_sb.append(group_products(3, mf3, "zg"))
+        zm = zm + [member_products(*parts[k], "turned") for k in range(2, 5)]
 
         y_rows = out_0.rearrange("(p t) j -> p t j", t=PACK)
         word_rows = out_1[0].rearrange("p c r -> p (c r)").bitcast(I32)
         y_plane = held.tile([P, J], U8, name="y_plane", align_bytes=64)
-        groups = CHUNK // MEMBERS
+
+        def add_groups(y_part, k, zg_part):
+            slices, cols = parts[k]
+            if k >= len(zm):
+                zm.append(member_products(slices, cols, "turned" if k == 7 else "zm"))
+            groups = (cols.stop - cols.start) // MEMBERS
+            nc.vector.tensor_tensor(
+                out=y_part.rearrange("p t (b i) -> p t b i", i=MEMBERS),
+                in0=zm[k][:].rearrange("p t (b i) -> p t b i", i=MEMBERS),
+                in1=zg_part.unsqueeze(3).to_broadcast([P, len(slices), groups, MEMBERS]),
+                op=ADD,
+            )
+
+        def quantise_result(y_part, cols, codes):
+            rounded = held.tile([P, CHUNK, PACK], BF16, name="rounded%d" % cols.start, align_bytes=64)
+            copy = nc.vector.tensor_copy if cols.stop == J else nc.scalar.copy
+            copy(
+                out=rounded[:].rearrange("p (g i) t -> p g t i", i=4),
+                in_=y_part.rearrange("p t (g i) -> p g t i", i=4),
+            )
+            nc.vector.quantize_mx(
+                out=codes.bitcast(FP8X4), scales=y_plane[:, cols], in_=rounded[:].rearrange("p j t -> p (j t)")
+            )
+
         for q in range(4):
-            y = held.tile([P, 2, PACK, CHUNK], F32, name="y%d" % q)
-            y_codes = held.tile([P, 2 * CHUNK], I32, name="y_codes%d" % q, align_bytes=64)
+            cols = slice(wide * q, wide * (q + 1))
+            y_codes = held.tile([P, wide], I32, name="y_codes%d" % q, align_bytes=64)
+            if q < 3:
+                y = held.tile([P, PACK, wide], F32, name="y%d" % q)
+                for u in range(2):
+                    add_groups(y[:, 2 * u : 2 * u + 2, :], 2 * q + u, zg_sb[q][:, 2 * u : 2 * u + 2, :])
+                nc.sync.dma_start(out=y_rows[:, :, cols], in_=y[:])
             for s in range(2):
-                c = 2 * q + s
-                zm = member_products(c)
-                nc.vector.tensor_tensor(
-                    out=y[:, s, :, :].rearrange("p t (b i) -> p t b i", i=MEMBERS),
-                    in0=zm[:].rearrange("p t (b i) -> p t b i", i=MEMBERS),
-                    in1=zg_sb[q][:, :, s * groups : (s + 1) * groups]
-                    .unsqueeze(3)
-                    .to_broadcast([P, PACK, groups, MEMBERS]),
-                    op=ADD,
-                )
-                nc.sync.dma_start(out=y_rows[:, :, CHUNK * c : CHUNK * (c + 1)], in_=y[:, s, :, :])
-                rounded = held.tile([P, CHUNK, PACK], BF16, name="rounded%d" % c, align_bytes=64)
-                nc.scalar.copy(
-                    out=rounded[:].rearrange("p (g i) t -> p g t i", i=4),
-                    in_=y[:, s, :, :].rearrange("p t (g i) -> p g t i", i=4),
-                )
-                nc.vector.quantize_mx(
-                    out=y_codes[:, s * CHUNK : (s + 1) * CHUNK].bitcast(FP8X4),
-                    scales=y_plane[:, CHUNK * c : CHUNK * (c + 1)],
-                    in_=rounded[:].rearrange("p j t -> p (j t)"),
-                )
-            nc.sync.dma_start(out=word_rows[:, 2 * CHUNK * q : 2 * CHUNK * (q + 1)], in_=y_codes[:])
+                part = slice(cols.start + CHUNK * s, cols.start + CHUNK * (s + 1))
+                if q < 3:
+                    y_part = y[:, :, CHUNK * s : CHUNK * (s + 1)]
+                else:
+                    y_last = held.tile([P, PACK, CHUNK], F32, name="y_last%d" % s)
+                    y_part = y_last[:]
+                    groups = CHUNK // MEMBERS
+                    add_groups(y_part, 2 * q + s, zg_sb[q][:, :, groups * s : groups * (s + 1)])
+                    nc.sync.dma_start(out=y_rows[:, :, part], in_=y_part)
+                quantise_result(y_part, part, y_codes[:, CHUNK * s : CHUNK * (s + 1)])
+            nc.sync.dma_start(out=word_rows[:, cols], in_=y_codes[:])
         for quad in range(4):
             queue = nc.sync if quad % 2 == 0 else nc.scalar
             queue.dma_start(

@@ -150,7 +150,8 @@ def tile_list_group_mean_and_members_pl_kernel(
             return mf
 
         def group_products(q, mf, bank):
-            codes = held.tile([P, QUARTER], I32, name="mf_codes%d" % q, align_bytes=64)
+            tag = "zg_sb0" if q == 2 else "mf_codes%d" % q
+            codes = held.tile([P, QUARTER], I32, name="mf_codes%d" % q, tag=tag, align_bytes=64)
             plane = held.tile([P, QUARTER], U8, name="mf_plane%d" % q, align_bytes=64)
             nc.vector.quantize_mx(
                 out=codes[:].bitcast(FP8X4), scales=plane[:], in_=mf[:].rearrange("p b t -> p (b t)")
@@ -166,7 +167,7 @@ def tile_list_group_mean_and_members_pl_kernel(
                     start=True,
                     stop=True,
                 )
-            staged = held.tile([P, PACK, QUARTER], F32, name="zg_sb%d" % q)
+            staged = held.tile([P, PACK, QUARTER], F32, name="zg_sb%d" % q, align_bytes=64)
             nc.scalar.copy(out=staged[:], in_=zg[:])
             return staged
 
@@ -181,8 +182,6 @@ def tile_list_group_mean_and_members_pl_kernel(
         mf2 = pick_last(2)
         zg_sb.append(group_products(1, mf1, "turned"))
         mf3 = pick_last(3)
-        zg_sb.append(group_products(2, mf2, "zg"))
-        zg_sb.append(group_products(3, mf3, "zg"))
         zm = zm + [member_products(*parts[k], "turned") for k in range(2, 5)]
 
         y_rows = out_0.rearrange("(p t) j -> p t j", t=PACK)
@@ -219,7 +218,10 @@ def tile_list_group_mean_and_members_pl_kernel(
                 y = held.tile([P, PACK, wide], F32, name="y%d" % q)
                 for u in range(2):
                     add_groups(y[:, 2 * u : 2 * u + 2, :], 2 * q + u, zg_sb[q][:, 2 * u : 2 * u + 2, :])
-                nc.sync.dma_start(out=y_rows[:, :, cols], in_=y[:])
+                    nc.sync.dma_start(out=y_rows[:, 2 * u : 2 * u + 2, cols], in_=y[:, 2 * u : 2 * u + 2, :])
+            if q == 0:
+                zg_sb.append(group_products(2, mf2, "zg"))
+                zg_sb.append(group_products(3, mf3, "zg"))
             for s in range(2):
                 part = slice(cols.start + CHUNK * s, cols.start + CHUNK * (s + 1))
                 if q < 3:

from contextlib import ExitStack

import concourse.mybir as mybir
from concourse.masks import make_identity

K, T, J, B, N = 512, 2048, 1024, 256, 512
FLOPS = 2 * K * N * (J + B)

F32 = mybir.dt.float32
BF16 = mybir.dt.bfloat16
I32 = mybir.dt.int32
U16 = mybir.dt.uint16
U8 = mybir.dt.uint8
FP8X4 = mybir.dt.float8_e4m3fn_x4
FP4X4 = mybir.dt.float4_e2m1fn_x4
ADD = mybir.AluOpType.add
COPY = mybir.ActivationFunctionType.Copy
AXIS_X = mybir.AxisListType.X

P = 128
PACK = 4
MEMBERS = J // B
HALF = B // 2
QUARTER = B // 4
CHUNK = 128
BANKS = {"turned": 3, "zm": 2, "zg": 2}


def load_scale_rows(queue, plane, scales):
    for quad in range(4):
        queue.dma_start(
            out=plane[32 * quad : 32 * quad + 4, :].bitcast(I32),
            in_=scales[0, 4 * quad : 4 * quad + 4, :].bitcast(I32),
        )


def tile_list_group_mean_and_members_pl_kernel(
    tc, xf, wg_words, wg_scales, xq_words, xq_scales, wm_words, wm_scales, offs, out_0, out_1, out_2
):
    nc = tc.nc
    with ExitStack() as ctx:
        held = ctx.enter_context(tc.tile_pool(name="held", bufs=1))
        psum = ctx.enter_context(tc.psum_pool(name="psum", bufs=1))

        offsets = held.tile([P, J // 16], U16, name="offsets")
        nc.sync.dma_start(offsets[:], offs)

        wg_sraw = held.tile([P, N], U8, name="wg_sraw", align_bytes=64)
        wm_sraw = held.tile([P, N], U8, name="wm_sraw", align_bytes=64)
        xq_plane = held.tile([P, J], U8, name="xq_plane", align_bytes=64)
        for plane in (wm_sraw, wg_sraw, xq_plane):
            nc.gpsimd.memset(plane[:].bitcast(I32), 0)
        ident = held.tile([P, P], F32, name="ident")
        make_identity(nc, ident[:])

        x_rows = xf.rearrange("(p t) c -> p t c", t=PACK)
        x = [held.tile([P, T], F32, name="x%d" % t, align_bytes=64) for t in range(PACK)]
        wm_raw = held.tile([P, N], I32, name="wm_raw", align_bytes=64)
        wg_raw = held.tile([P, N], I32, name="wg_raw", align_bytes=64)
        xq = held.tile([P, 2 * J], U8, name="xq", align_bytes=64)

        nc.sync.dma_start(out=x[0][:], in_=x_rows[:, 0, :])
        load_scale_rows(nc.sync, wm_sraw, wm_scales)
        nc.sync.dma_start(out=x[1][:], in_=x_rows[:, 1, :])
        nc.sync.dma_start(out=wm_raw[:], in_=wm_words[0].rearrange("p n t -> p (n t)").bitcast(I32))
        load_scale_rows(nc.sync, wg_sraw, wg_scales)
        nc.sync.dma_start(out=xq[:].bitcast(I32), in_=xq_words[0].bitcast(I32))
        nc.sync.dma_start(out=x[2][:], in_=x_rows[:, 2, :])
        load_scale_rows(nc.sync, xq_plane, xq_scales)
        nc.sync.dma_start(out=x[3][:], in_=x_rows[:, 3, :])
        nc.sync.dma_start(out=wg_raw[:], in_=wg_words[0].rearrange("p n t -> p (n t)").bitcast(I32))

        def deal(raw, dtype, name, tag):
            dealt = held.tile([P, PACK, P], dtype, name=name, tag=tag, align_bytes=64)
            if dtype == U8:
                nc.vector.tensor_copy(out=dealt[:], in_=raw[:].rearrange("p (m t) -> p t m", t=PACK))
            else:
                nc.vector.tensor_copy(
                    out=dealt[:].rearrange("p t m -> p m t"), in_=raw[:].rearrange("p (m t) -> p m t", t=PACK)
                )
            return dealt

        sums = [held.tile([P, PACK, HALF], F32, name="sums%d" % h) for h in range(2)]

        def sum_on_tensor(t, h):
            name = "picked%d%d" % (t, h)
            tag = "wm_raw" if (t, h) == (2, 0) else name
            picked = held.tile([P, HALF, MEMBERS], F32, name=name, tag=tag, align_bytes=64)
            cols = HALF * MEMBERS // 16
            nc.vector.tensor_copy(
                out=picked[:].rearrange("p b i -> p (b i)"),
                in_=x[t][:].indirect(offsets[:, h * cols : (h + 1) * cols]),
            )
            by_member = picked[:].rearrange("p b i -> p i b")
            if t < 2:
                parted = held.tile([P, MEMBERS, HALF], F32, name="parted%d%d" % (t, h))
                nc.scalar.copy(out=parted[:].rearrange("p i b -> p b i"), in_=picked[:])
                by_member = parted[:]
            turned = psum.tile([P, P], F32, name="turned", bufs=3)
            for i in range(MEMBERS):
                nc.tensor.matmul(
                    turned[:], by_member[:, i, :], ident[:], start=(i == 0), stop=(i == MEMBERS - 1), is_transpose=True
                )
            turned_sb = held.tile([P, P], F32, name="turned_sb%d%d" % (t, h))
            nc.scalar.activation(out=turned_sb[:], in_=turned[:], func=COPY)
            return turned_sb

        def turn_back(h, planes):
            back = psum.tile([P, PACK - 1, P], F32, name="back%d" % h, tag="turned", bufs=3)
            for t in range(PACK - 1):
                nc.tensor.transpose(back[:, t, :], planes[t][:], ident[:])
            nc.scalar.copy(out=sums[h][:, 0 : PACK - 1, :], in_=back[:])

        early = [[sum_on_tensor(t, h) for h in range(2)] for t in range(2)]
        wm_plane = deal(wm_sraw, U8, "wm_plane", "x0")
        wm = deal(wm_raw, I32, "wm", "x1")
        wg_plane = deal(wg_sraw, U8, "wg_plane", "picked01")
        for h in range(2):
            turn_back(h, [early[0][h], early[1][h], sum_on_tensor(2, h)])

        def member_products(slices, cols, tag):
            width = cols.stop - cols.start
            zm = psum.tile([P, len(slices), width], F32, name="zm", tag=tag, bufs=BANKS[tag])
            for k, t in enumerate(slices):
                nc.tensor.matmul_mx(
                    out=zm[:, k, :],
                    lhsT=wm[:, t, :].bitcast(FP8X4),
                    lhsT_scale=wm_plane[:, t, :],
                    rhs=xq[:, 2 * cols.start : 2 * cols.stop].bitcast(FP4X4),
                    rhs_scale=xq_plane[:, cols],
                    start=True,
                    stop=True,
                )
            return zm

        def pick_last(q):
            tag = "mf0" if q == 3 else "last%d" % q
            picked = held.tile([P, QUARTER, MEMBERS], F32, name="last%d" % q, tag=tag, align_bytes=64)
            cols = QUARTER * MEMBERS // 16
            nc.vector.tensor_copy(
                out=picked[:].rearrange("p b i -> p (b i)"),
                in_=x[3][:].indirect(offsets[:, q * cols : (q + 1) * cols]),
            )
            mine = slice(QUARTER * (q % 2), QUARTER * (q % 2 + 1))
            nc.vector.tensor_reduce(out=sums[q // 2][:, 3, mine], in_=picked[:], axis=AXIS_X, op=ADD)
            mf = held.tile([P, QUARTER, PACK], BF16, name="mf%d" % q, align_bytes=64)
            nc.scalar.activation(
                out=mf[:], in_=sums[q // 2][:, :, mine].rearrange("p t b -> p b t"), func=COPY, scale=2.0 / MEMBERS
            )
            return mf

        def group_products(q, mf, bank):
            tag = "zg_sb0" if q == 2 else "mf_codes%d" % q
            codes = held.tile([P, QUARTER], I32, name="mf_codes%d" % q, tag=tag, align_bytes=64)
            plane = held.tile([P, QUARTER], U8, name="mf_plane%d" % q, align_bytes=64)
            nc.vector.quantize_mx(
                out=codes[:].bitcast(FP8X4), scales=plane[:], in_=mf[:].rearrange("p b t -> p (b t)")
            )
            zg = psum.tile([P, PACK, QUARTER], F32, name="zg", tag=bank, bufs=BANKS[bank])
            for t in range(PACK):
                nc.tensor.matmul_mx(
                    out=zg[:, t, :],
                    lhsT=wg[:, t, :].bitcast(FP8X4),
                    lhsT_scale=wg_plane[:, t, :],
                    rhs=codes[:].bitcast(FP8X4),
                    rhs_scale=plane[:],
                    start=True,
                    stop=True,
                )
            staged = held.tile([P, PACK, QUARTER], F32, name="zg_sb%d" % q, align_bytes=64)
            nc.scalar.copy(out=staged[:], in_=zg[:])
            return staged

        wide = 2 * CHUNK
        parts = [((2 * u, 2 * u + 1), slice(wide * q, wide * (q + 1))) for q in range(3) for u in range(2)]
        parts = parts + [(range(PACK), slice(3 * wide + CHUNK * s, 3 * wide + CHUNK * (s + 1))) for s in range(2)]
        zm = [member_products(*parts[k], "zm") for k in range(2)]
        mf0 = pick_last(0)
        mf1 = pick_last(1)
        wg = deal(wg_raw, I32, "wg", "last1")
        zg_sb = [group_products(0, mf0, "turned")]
        mf2 = pick_last(2)
        zg_sb.append(group_products(1, mf1, "turned"))
        mf3 = pick_last(3)
        zm = zm + [member_products(*parts[k], "turned") for k in range(2, 5)]

        y_rows = out_0.rearrange("(p t) j -> p t j", t=PACK)
        word_rows = out_1[0].rearrange("p c r -> p (c r)").bitcast(I32)
        y_plane = held.tile([P, J], U8, name="y_plane", align_bytes=64)

        def add_groups(y_part, k, zg_part):
            slices, cols = parts[k]
            if k >= len(zm):
                zm.append(member_products(slices, cols, "turned" if k == 7 else "zm"))
            groups = (cols.stop - cols.start) // MEMBERS
            nc.vector.tensor_tensor(
                out=y_part.rearrange("p t (b i) -> p t b i", i=MEMBERS),
                in0=zm[k][:].rearrange("p t (b i) -> p t b i", i=MEMBERS),
                in1=zg_part.unsqueeze(3).to_broadcast([P, len(slices), groups, MEMBERS]),
                op=ADD,
            )

        def quantise_result(y_part, cols, codes):
            rounded = held.tile([P, CHUNK, PACK], BF16, name="rounded%d" % cols.start, align_bytes=64)
            copy = nc.vector.tensor_copy if cols.stop == J else nc.scalar.copy
            copy(
                out=rounded[:].rearrange("p (g i) t -> p g t i", i=4),
                in_=y_part.rearrange("p t (g i) -> p g t i", i=4),
            )
            nc.vector.quantize_mx(
                out=codes.bitcast(FP8X4), scales=y_plane[:, cols], in_=rounded[:].rearrange("p j t -> p (j t)")
            )

        for q in range(4):
            cols = slice(wide * q, wide * (q + 1))
            y_codes = held.tile([P, wide], I32, name="y_codes%d" % q, align_bytes=64)
            if q < 3:
                y = held.tile([P, PACK, wide], F32, name="y%d" % q)
                for u in range(2):
                    add_groups(y[:, 2 * u : 2 * u + 2, :], 2 * q + u, zg_sb[q][:, 2 * u : 2 * u + 2, :])
                    nc.sync.dma_start(out=y_rows[:, 2 * u : 2 * u + 2, cols], in_=y[:, 2 * u : 2 * u + 2, :])
            if q == 0:
                zg_sb.append(group_products(2, mf2, "zg"))
                zg_sb.append(group_products(3, mf3, "zg"))
            for s in range(2):
                part = slice(cols.start + CHUNK * s, cols.start + CHUNK * (s + 1))
                if q < 3:
                    y_part = y[:, :, CHUNK * s : CHUNK * (s + 1)]
                else:
                    y_last = held.tile([P, PACK, CHUNK], F32, name="y_last%d" % s)
                    y_part = y_last[:]
                    groups = CHUNK // MEMBERS
                    add_groups(y_part, 2 * q + s, zg_sb[q][:, :, groups * s : groups * (s + 1)])
                    nc.sync.dma_start(out=y_rows[:, :, part], in_=y_part)
                quantise_result(y_part, part, y_codes[:, CHUNK * s : CHUNK * (s + 1)])
            nc.sync.dma_start(out=word_rows[:, cols], in_=y_codes[:])
        for quad in range(4):
            queue = nc.sync if quad % 2 == 0 else nc.scalar
            queue.dma_start(
                out=out_2[0, 4 * quad : 4 * quad + 4, :].bitcast(I32),
                in_=y_plane[32 * quad : 32 * quad + 4, :].bitcast(I32),
            )
